import numpy as np
import ml_dtypes


def mxq(x, axis, fmt="e4m3"):
    dtype, down = {"e4m3": (ml_dtypes.float8_e4m3fn, 7), "e5m2": (ml_dtypes.float8_e5m2, 14)}[fmt]
    v = np.moveaxis(np.asarray(x, np.float32).astype(ml_dtypes.bfloat16).astype(np.float64), axis, -1)
    blocks = v.reshape(v.shape[:-1] + (-1, 32))
    amax = np.abs(blocks).max(-1, keepdims=True)
    byte = np.maximum(np.where(amax > 0, np.frexp(amax)[1] - 1 + 127, 0) - down, 1)
    scale = np.exp2(byte - 127.0)
    codes = (blocks / scale).astype(np.float32).astype(dtype).astype(np.float64)
    return np.moveaxis((codes * scale).reshape(v.shape), -1, axis)


WIDE = False


def mx_kscale(k):
    if not WIDE:
        return np.ones(k)
    levels = np.array([18, -18])
    if k % 512:
        return np.exp2(np.random.permutation(np.resize(levels, k // 32))).repeat(32)
    a = np.empty((k // 512, 16))
    for p in range(k // 512):
        a[p, :8] = np.random.permutation(np.resize(levels, 8))
        for g in range(8):
            far = levels[np.abs(levels - a[p, g]) >= 10]
            a[p, g + 8] = far[np.random.randint(len(far))]
    return np.exp2(a.ravel()).repeat(32)


def f64(x):
    return np.asarray(x).astype(np.float64)


def striped(idx):
    return np.tile(np.asarray(idx).reshape(-1, 16).T, (8, 1)).astype(np.uint16)


def unstriped(offs):
    return offs[:16].T.reshape(-1).astype(np.int64)


def setup_inputs():
    n = np.random.standard_normal
    uni = np.random.uniform
    dst = np.random.permutation(np.repeat(np.arange(512), 2))
    inn = np.argsort(dst, kind="stable")
    src = np.random.permutation(np.repeat(np.arange(512), 2))
    outg = np.argsort(src, kind="stable")
    f_m = mx_kscale(512)
    return {
        "hT": (n((512, 512))).astype(np.float32),
        "W": (n((512, 512)) / np.sqrt(512) * f_m[:, None]).astype(np.float32),
        "dyT": (n((512, 512)) / f_m[:, None]).astype(np.float32),
        "sc": np.tile(n(1024), (128, 1)).astype(np.float32),
        "dstoffs": striped(dst),
        "innoffs": striped(inn),
        "soffs": striped(src),
        "ooffs": striped(outg),
    }


def reference(hT, W, dyT, sc, dstoffs, innoffs, soffs, ooffs):
    dst = unstriped(dstoffs)
    inn = unstriped(innoffs)
    src = unstriped(soffs)
    outg = unstriped(ooffs)
    e = np.exp(f64(sc)[:1])
    es = e[:, inn]
    den = es.reshape(1, 512, 2).sum(-1)
    dn = den[:, dst]
    al = e / dn
    u = mxq(f64(W), 0, "e4m3").T @ mxq(f64(dyT), 0, "e5m2")
    ud = u[:, dst]
    t = al * ud
    to = t[:, outg]
    out_0 = to.reshape(512, 512, 2).sum(-1)
    hs = f64(hT)[:, src]
    q = ud * hs
    qt = q.T
    da = (qt).sum(-1, keepdims=True)
    dar = da.T
    w = al * dar
    wi = w[:, inn]
    sw = wi.reshape(1, 512, 2).sum(-1)
    sb = sw[:, dst]
    out_1 = al * (dar - sb)
    return out_0, out_1

@@ -1,0 +1,235 @@
+from contextlib import ExitStack
+
+import concourse.mybir as mybir
+from concourse.masks import make_identity
+
+F32 = mybir.dt.float32
+BF16 = mybir.dt.bfloat16
+U32 = mybir.dt.uint32
+U16 = mybir.dt.uint16
+U8 = mybir.dt.uint8
+E4M3 = mybir.dt.float8_e4m3fn_x4
+E5M2 = mybir.dt.float8_e5m2_x4
+ACT = mybir.ActivationFunctionType
+MULT = mybir.AluOpType.mult
+ADD = mybir.AluOpType.add
+
+P = 128
+NODES = 512
+EDGES = 1024
+HALF = EDGES // 2
+BLOCKS = 4
+SPARE = 8
+FLOPS = 2 * 512 * 512 * 512
+
+
+def tile_attend_ggattn_kernel(tc, hT, W, dyT, sc, dstoffs, innoffs, soffs, ooffs, out_0, out_1):
+    nc = tc.nc
+    with ExitStack() as ctx:
+        keep = ctx.enter_context(tc.tile_pool(name="keep", bufs=1))
+        psum = ctx.enter_context(tc.psum_pool(name="psum", bufs=1))
+
+        def half_list(offs, a):
+            return offs[:, a * (HALF // 16):(a + 1) * (HALF // 16)]
+
+        def half(t, a):
+            return t[:, a * HALF:(a + 1) * HALF]
+
+        def node_window(name):
+            t = keep.tile([P, NODES + SPARE], F32, name=name)
+            nc.vector.memset(t[:, NODES:], 0.0)
+            return t
+
+        src_l = keep.tile([P, EDGES // 16], U16, name="src_l")
+        inn_l = keep.tile([P, EDGES // 16], U16, name="inn_l")
+        dst_l = keep.tile([P, EDGES // 16], U16, name="dst_l")
+        out_l = keep.tile([P, EDGES // 16], U16, name="out_l")
+
+        warm = keep.tile([P, 8], F32, name="warm")
+        nc.vector.memset(warm[:], 0.0)
+        warm2 = keep.tile([P, 8], F32, name="warm2")
+        nc.scalar.activation(warm2[:], warm[:], ACT.Exp)
+
+        e = keep.tile([P, EDGES], F32, name="e")
+        nc.vector.memset(e[:], 0.0)
+        h = [node_window("h%d" % j) for j in range(BLOCKS)]
+        u = [node_window("u%d" % j) for j in range(BLOCKS)]
+        den = node_window("den")
+        sw = node_window("sw")
+        ident = keep.tile([P, P], F32, name="ident")
+        make_identity(nc, ident[:])
+        o1col = keep.tile([P, P], F32, name="o1col")
+        nc.gpsimd.memset(o1col[:], 0.0)
+
+        sc_row = keep.tile([1, EDGES], F32, name="sc_row")
+        dy_raw = keep.tile([P, 4, NODES], F32, name="dy_raw")
+        w_raw = [keep.tile([P, 4, P], F32, name="w_raw%d" % j) for j in range(BLOCKS)]
+        nc.sync.dma_start(sc_row[:], sc[0:1, :])
+        nc.sync.dma_start(inn_l[:], innoffs)
+        nc.sync.dma_start(dst_l[:], dstoffs)
+        nc.sync.dma_start(dy_raw[:], dyT.rearrange("(p j) x -> p j x", j=4))
+        Wv = W.rearrange("(p j) d -> p j d", j=4)
+        for j in range(BLOCKS):
+            nc.sync.dma_start(w_raw[j][:], Wv[:, :, j * P:(j + 1) * P])
+        nc.sync.dma_start(src_l[:], soffs)
+        for j in range(BLOCKS):
+            nc.sync.dma_start(h[j][:, :NODES], hT[j * P:(j + 1) * P, :])
+        nc.sync.dma_start(out_l[:], ooffs)
+
+        def new_bank(tag):
+            return psum.tile([P, 4, P], F32, name="bank", tag=tag)
+
+        def to_columns(row, tag):
+            bank = new_bank(tag)
+            for b in range(4):
+                nc.tensor.transpose(bank[:, b, :], row[:, b * P:(b + 1) * P], ident[:])
+            return bank
+
+        def to_row(row, col, j0, n, tag):
+            bank = new_bank(tag)
+            for b in range(n):
+                nc.tensor.transpose(bank[:, b, :], col[:, j0 + b:j0 + b + 1].to_broadcast([P, P]), ident[:])
+            nc.scalar.copy(row[:, j0 * P:(j0 + n) * P], bank[:, :n, :].rearrange("p b c -> p (b c)"))
+
+        def pair_sum(dst, gathered):
+            nc.vector.tensor_tensor(dst, gathered[:, 0::2], gathered[:, 1::2], ADD)
+
+        def pair_columns(gathered, tag):
+            bank = new_bank(tag)
+            for b in range(2):
+                for r in range(2):
+                    nc.tensor.matmul(bank[:, b, :], gathered[:, 2 * P * b + r:2 * P * (b + 1):2], ident[:],
+                                     is_transpose=True, start=(r == 0), stop=(r == 1))
+            return bank
+
+        def look_up(dst, window, offs, a):
+            nc.vector.tensor_copy(dst, window[:].indirect(half_list(offs, a)))
+
+        nc.scalar.activation(e[0:1, :], sc_row[:], ACT.Exp)
+        e_col = keep.tile([P, 8], F32, name="e_col")
+        for a in range(2):
+            nc.scalar.copy(e_col[:, 4 * a:4 * a + 4], to_columns(half(e, a), "xy"[a])[:, :, 0])
+        es = keep.tile([P, EDGES], F32, name="es")
+        for a in range(2):
+            look_up(half(es, a), e, inn_l, a)
+        pair_sum(den[:, :NODES], es[:])
+
+        al_col = keep.tile([P, 8], F32, name="al_col")
+        nal_col = keep.tile([P, 8], F32, name="nal_col")
+        al = keep.tile([P, EDGES], F32, name="al")
+        dn0 = keep.tile([P, HALF], F32, name="dn0")
+        look_up(dn0[:], den, dst_l, 0)
+
+        dy_bf = keep.tile([P, NODES, 4], BF16, name="dy_bf", align_bytes=64)
+        nc.scalar.copy(dy_bf[:], dy_raw[:].rearrange("p j x -> p x j"))
+        dy_q = keep.tile([P, NODES], U32, name="dy_q", align_bytes=64)
+        dy_s = keep.tile([P, NODES], U8, name="dy_s", align_bytes=64)
+        nc.vector.quantize_mx(out=dy_q[:].bitcast(E5M2), scales=dy_s[:], in_=dy_bf[:].rearrange("p x j -> p (x j)"))
+
+        def product(j):
+            w_bf = keep.tile([P, P, 4], BF16, name="w_bf%d" % j, align_bytes=64)
+            nc.scalar.copy(w_bf[:], w_raw[j][:].rearrange("p j d -> p d j"))
+            w_q = keep.tile([P, P], U32, name="w_q%d" % j, align_bytes=64)
+            w_s = keep.tile([P, P], U8, name="w_s%d" % j, align_bytes=64)
+            nc.vector.quantize_mx(out=w_q[:].bitcast(E4M3), scales=w_s[:], in_=w_bf[:].rearrange("p d j -> p (d j)"))
+            acc = psum.tile([P, NODES], F32, name="acc", tag="u%d" % j)
+            nc.tensor.matmul_mx(out=acc[:], lhsT=w_q[:].bitcast(E4M3), lhsT_scale=w_s[:],
+                                rhs=dy_q[:].bitcast(E5M2), rhs_scale=dy_s[:], start=True, stop=True)
+            nc.scalar.copy(u[j][:, :NODES], acc[:])
+
+        def weights(a, dn, rdn_tag):
+            cols = slice(4 * a, 4 * a + 4)
+            rdn = keep.tile([P, 4], F32, name="rdn%d" % a, tag=rdn_tag, align_bytes=64)
+            nc.vector.reciprocal(rdn[:], to_columns(dn, "x")[:, :, 0])
+            nc.vector.tensor_tensor(al_col[:, cols], rdn[:], e_col[:, cols], MULT)
+            to_row(al, al_col, 4 * a, 4, "y")
+
+        product(0)
+        weights(0, dn0, "dy_bf")
+        dn1 = keep.tile([P, HALF], F32, name="dn1", tag="w_bf0", align_bytes=64)
+        look_up(dn1[:], den, dst_l, 1)
+        product(1)
+        weights(1, dn1, "rdn1")
+        for j in range(2, BLOCKS):
+            product(j)
+        nc.scalar.mul(nal_col[:], al_col[:], -1.0)
+
+        t = [keep.tile([P, EDGES], F32, name="t%d" % j) for j in range(BLOCKS)]
+        q = [keep.tile([P, EDGES], F32, name="q%d" % j) for j in range(BLOCKS)]
+        sums = [new_bank("qa"), new_bank("qb")]
+        for j in range(BLOCKS):
+            for a in range(2):
+                nc.vector.tensor_tensor(half(t[j], a), u[j][:].indirect(half_list(dst_l, a)), half(al, a), MULT)
+            for a in range(2):
+                nc.vector.tensor_tensor(half(q[j], a), h[j][:].indirect(half_list(src_l, a)), half(t[j], a), MULT)
+                for b in range(4):
+                    c0 = a * HALF + b * P
+                    nc.tensor.matmul(sums[a][:, b, :], q[j][:, c0:c0 + P], ident[:], is_transpose=True,
+                                     start=(j == 0 and b == 0), stop=(j == BLOCKS - 1 and b == 3))
+
+        w_col = keep.tile([P, 8], F32, name="w_col")
+        junk = keep.tile([P, P], F32, name="junk")
+        w_row = keep.tile([P, EDGES], F32, name="w_row")
+        for a in range(2):
+            for b in range(4):
+                nc.scalar.activation(junk[:], sums[a][:, b, :], ACT.Copy, accum_out=w_col[:, 4 * a + b:4 * a + b + 1])
+            if a == 0:
+                to_row(w_row, w_col, 0, 4, "u0")
+            else:
+                to_row(w_row, w_col, 4, 2, "x")
+                to_row(w_row, w_col, 6, 2, "y")
+
+        def store_half(j, a, res, queue):
+            queue.dma_start(out_0[j * P:(j + 1) * P, a * 256:(a + 1) * 256], res)
+
+        def finish(j, a, to):
+            turned = keep.tile([P, 2, P], F32, name="turned%d%d" % (j, a))
+            nc.scalar.copy(turned[:], pair_columns(to, "xy"[a])[:, :2, :])
+            bank = new_bank("q" + "ab"[a])
+            for b in range(2):
+                nc.tensor.transpose(bank[:, b, :], turned[:, b, :], ident[:])
+            res = keep.tile([P, 2 * P], F32, name="res%d%d" % (j, a))
+            nc.scalar.copy(res[:], bank[:, :2, :].rearrange("p b c -> p (b c)"))
+            store_half(j, a, res[:], nc.sync)
+
+        def node_halves(pieces, tag):
+            to = keep.tile([P, len(pieces) * HALF], F32, name="to", tag=tag)
+            for i, (j, a) in enumerate(pieces):
+                look_up(half(to, i), t[j], out_l, a)
+            return to
+
+        first = [(0, 0), (0, 1), (1, 0)]
+        to = node_halves(first, "first")
+        for i, (j, a) in enumerate(first):
+            finish(j, a, half(to, i))
+        wi = keep.tile([P, EDGES], F32, name="wi")
+        sw_col = keep.tile([P, 4], F32, name="sw_col")
+        for a in range(2):
+            look_up(half(wi, a), w_row, inn_l, a)
+            nc.scalar.copy(sw_col[:, 2 * a:2 * a + 2], pair_columns(half(wi, a), "u%d" % (1 + a))[:, :2, 0])
+        to_row(sw, sw_col, 0, 2, "u3")
+        to_row(sw, sw_col, 2, 1, "x")
+        to_row(sw, sw_col, 3, 1, "y")
+        second = [(1, 1), (2, 0)]
+        to = node_halves(second, "w_row")
+        for i, (j, a) in enumerate(second):
+            finish(j, a, half(to, i))
+        sb = keep.tile([P, EDGES], F32, name="sb")
+        for a in range(2):
+            look_up(half(sb, a), sw, dst_l, a)
+            bank = to_columns(half(sb, a), "u%d" % a)
+            for b in range(4):
+                j = 4 * a + b
+                nc.scalar.activation(o1col[:, j:j + 1], bank[:, b, 0:1], ACT.Identity,
+                                     scale=nal_col[:, j:j + 1], bias=w_col[:, j:j + 1])
+        bank = new_bank("u2")
+        nc.tensor.transpose(bank[:, 0, :], o1col[:], ident[:])
+        o1row = keep.tile([8, P], F32, name="o1row")
+        nc.scalar.copy(o1row[:], bank[0:8, 0, :])
+        nc.sync.dma_start(out_1.rearrange("o (j p) -> (o j) p", p=P), o1row[:])
+        to = node_halves([(2, 1), (3, 0), (3, 1)], "sw")
+        finish(2, 1, half(to, 0))
+        res = keep.tile([P, NODES], F32, name="res3")
+        for a in range(2):
+            pair_sum(res[:, a * 256:(a + 1) * 256], half(to, 1 + a))
+            store_half(3, a, res[:, a * 256:(a + 1) * 256], nc.sync)

@@ -61,16 +61,19 @@ def tile_attend_ggattn_kernel(tc, hT, W, dyT, sc, dstoffs, innoffs, soffs, ooffs
         o1col = keep.tile([P, P], F32, name="o1col")
         nc.gpsimd.memset(o1col[:], 0.0)
 
-        sc_row = keep.tile([1, EDGES], F32, name="sc_row")
-        dy_raw = keep.tile([P, 4, NODES], F32, name="dy_raw")
-        w_raw = [keep.tile([P, 4, P], F32, name="w_raw%d" % j) for j in range(BLOCKS)]
+        sc_row = keep.tile([1, EDGES], F32, name="sc_row", tag="dy_bf", align_bytes=64)
+        dy_raw = [keep.tile([P, 4, 256], F32, name="dy_raw%d" % a) for a in range(2)]
+        w_parts = [(0, 1), (1, 1), (2, 2)]
+        w_raw = [keep.tile([P, 4, n * P], F32, name="w_raw%d" % j) for j, n in w_parts]
         nc.sync.dma_start(sc_row[:], sc[0:1, :])
         nc.sync.dma_start(inn_l[:], innoffs)
         nc.sync.dma_start(dst_l[:], dstoffs)
-        nc.sync.dma_start(dy_raw[:], dyT.rearrange("(p j) x -> p j x", j=4))
+        dyv = dyT.rearrange("(p j) x -> p j x", j=4)
+        for a in range(2):
+            nc.sync.dma_start(dy_raw[a][:], dyv[:, :, a * 256:(a + 1) * 256])
         Wv = W.rearrange("(p j) d -> p j d", j=4)
-        for j in range(BLOCKS):
-            nc.sync.dma_start(w_raw[j][:], Wv[:, :, j * P:(j + 1) * P])
+        for i, (j, n) in enumerate(w_parts):
+            nc.sync.dma_start(w_raw[i][:], Wv[:, :, j * P:(j + n) * P])
         nc.sync.dma_start(src_l[:], soffs)
         for j in range(BLOCKS):
             nc.sync.dma_start(h[j][:, :NODES], hT[j * P:(j + 1) * P, :])
@@ -94,21 +97,11 @@ def tile_attend_ggattn_kernel(tc, hT, W, dyT, sc, dstoffs, innoffs, soffs, ooffs
         def pair_sum(dst, gathered):
             nc.vector.tensor_tensor(dst, gathered[:, 0::2], gathered[:, 1::2], ADD)
 
-        def pair_columns(gathered, tag):
-            bank = new_bank(tag)
-            for b in range(2):
-                for r in range(2):
-                    nc.tensor.matmul(bank[:, b, :], gathered[:, 2 * P * b + r:2 * P * (b + 1):2], ident[:],
-                                     is_transpose=True, start=(r == 0), stop=(r == 1))
-            return bank
-
         def look_up(dst, window, offs, a):
             nc.vector.tensor_copy(dst, window[:].indirect(half_list(offs, a)))
 
         nc.scalar.activation(e[0:1, :], sc_row[:], ACT.Exp)
-        e_col = keep.tile([P, 8], F32, name="e_col")
-        for a in range(2):
-            nc.scalar.copy(e_col[:, 4 * a:4 * a + 4], to_columns(half(e, a), "xy"[a])[:, :, 0])
+        e_banks = [to_columns(half(e, a), "q" + "ab"[a]) for a in range(2)]
         es = keep.tile([P, EDGES], F32, name="es")
         for a in range(2):
             look_up(half(es, a), e, inn_l, a)
@@ -117,103 +110,137 @@ def tile_attend_ggattn_kernel(tc, hT, W, dyT, sc, dstoffs, innoffs, soffs, ooffs
         al_col = keep.tile([P, 8], F32, name="al_col")
         nal_col = keep.tile([P, 8], F32, name="nal_col")
         al = keep.tile([P, EDGES], F32, name="al")
-        dn0 = keep.tile([P, HALF], F32, name="dn0")
-        look_up(dn0[:], den, dst_l, 0)
 
         dy_bf = keep.tile([P, NODES, 4], BF16, name="dy_bf", align_bytes=64)
-        nc.scalar.copy(dy_bf[:], dy_raw[:].rearrange("p j x -> p x j"))
+        for a in range(2):
+            nc.scalar.copy(dy_bf[:, a * 256:(a + 1) * 256, :], dy_raw[a][:].rearrange("p j x -> p x j"))
         dy_q = keep.tile([P, NODES], U32, name="dy_q", align_bytes=64)
         dy_s = keep.tile([P, NODES], U8, name="dy_s", align_bytes=64)
         nc.vector.quantize_mx(out=dy_q[:].bitcast(E5M2), scales=dy_s[:], in_=dy_bf[:].rearrange("p x j -> p (x j)"))
 
-        def product(j):
-            w_bf = keep.tile([P, P, 4], BF16, name="w_bf%d" % j, align_bytes=64)
-            nc.scalar.copy(w_bf[:], w_raw[j][:].rearrange("p j d -> p d j"))
-            w_q = keep.tile([P, P], U32, name="w_q%d" % j, align_bytes=64)
-            w_s = keep.tile([P, P], U8, name="w_s%d" % j, align_bytes=64)
+        def product(j0, n, tag):
+            w_bf = keep.tile([P, n * P, 4], BF16, name="w_bf%d" % j0, tag=tag, align_bytes=64)
+            nc.scalar.copy(w_bf[:], w_raw[j0][:].rearrange("p j d -> p d j"))
+            w_q = keep.tile([P, n * P], U32, name="w_q%d" % j0, align_bytes=64)
+            w_s = keep.tile([P, n * P], U8, name="w_s%d" % j0, align_bytes=64)
             nc.vector.quantize_mx(out=w_q[:].bitcast(E4M3), scales=w_s[:], in_=w_bf[:].rearrange("p d j -> p (d j)"))
-            acc = psum.tile([P, NODES], F32, name="acc", tag="u%d" % j)
-            nc.tensor.matmul_mx(out=acc[:], lhsT=w_q[:].bitcast(E4M3), lhsT_scale=w_s[:],
-                                rhs=dy_q[:].bitcast(E5M2), rhs_scale=dy_s[:], start=True, stop=True)
-            nc.scalar.copy(u[j][:, :NODES], acc[:])
+            for i in range(n):
+                cols = slice(i * P, (i + 1) * P)
+                acc = psum.tile([P, NODES], F32, name="acc", tag="u%d" % (j0 + i))
+                nc.tensor.matmul_mx(out=acc[:], lhsT=w_q[:, cols].bitcast(E4M3), lhsT_scale=w_s[:, cols],
+                                    rhs=dy_q[:].bitcast(E5M2), rhs_scale=dy_s[:], start=True, stop=True)
+                nc.scalar.copy(u[j0 + i][:, :NODES], acc[:])
+
+        product(0, 1, "w_bf0")
+        e_col = keep.tile([P, 8], F32, name="e_col", tag="w_raw0")
+        for a in range(2):
+            nc.scalar.copy(e_col[:, 4 * a:4 * a + 4], e_banks[a][:, :, 0])
+        dn0 = keep.tile([P, HALF], F32, name="dn0", tag="w_bf0", align_bytes=64)
+        look_up(dn0[:], den, dst_l, 0)
+        dn1 = keep.tile([P, HALF], F32, name="dn1")
+        look_up(dn1[:], den, dst_l, 1)
 
         def weights(a, dn, rdn_tag):
             cols = slice(4 * a, 4 * a + 4)
-            rdn = keep.tile([P, 4], F32, name="rdn%d" % a, tag=rdn_tag, align_bytes=64)
-            nc.vector.reciprocal(rdn[:], to_columns(dn, "x")[:, :, 0])
+            rdn = keep.tile([P, 4], F32, name="rdn%d" % a, tag=rdn_tag)
+            nc.vector.reciprocal(rdn[:], to_columns(dn, ("x", "u0")[a])[:, :, 0])
             nc.vector.tensor_tensor(al_col[:, cols], rdn[:], e_col[:, cols], MULT)
-            to_row(al, al_col, 4 * a, 4, "y")
+            to_row(al, al_col, 4 * a, 4, "yx"[a])
 
-        product(0)
-        weights(0, dn0, "dy_bf")
-        dn1 = keep.tile([P, HALF], F32, name="dn1", tag="w_bf0", align_bytes=64)
-        look_up(dn1[:], den, dst_l, 1)
-        product(1)
-        weights(1, dn1, "rdn1")
-        for j in range(2, BLOCKS):
-            product(j)
-        nc.scalar.mul(nal_col[:], al_col[:], -1.0)
+        weights(0, dn0, "den")
 
         t = [keep.tile([P, EDGES], F32, name="t%d" % j) for j in range(BLOCKS)]
         q = [keep.tile([P, EDGES], F32, name="q%d" % j) for j in range(BLOCKS)]
-        sums = [new_bank("qa"), new_bank("qb")]
-        for j in range(BLOCKS):
+        junk = keep.tile([P, P], F32, name="junk")
+
+        def scaled_look_up(dst, window, offs, other, c0, n):
+            nc.vector.tensor_tensor(dst[:, c0:c0 + n], window[:].indirect(offs[:, c0 // 16:(c0 + n) // 16]),
+                                    other[:, c0:c0 + n], MULT)
+
+        ud = keep.tile([P, HALF], F32, name="ud")
+        product(1, 1, "w_bf1")
+        product(2, 2, "w_bf2")
+        look_up(ud[:], u[0], dst_l, 0)
+        weights(1, dn1, "rdn1")
+        scaled_look_up(q[0], h[0], src_l, ud, 0, HALF)
+        nc.scalar.mul(nal_col[:], al_col[:], -1.0)
+        share_col = keep.tile([P, 4], F32, name="share_col")
+        nc.scalar.mul(share_col[:], al_col[:, 0:4], 1.0 / P)
+
+        bank = to_columns(ud, "y")
+        scaled = keep.tile([P, 4, P], F32, name="scaled")
+        for b in range(4):
+            nc.scalar.activation(scaled[:, b, :], bank[:, b, :], ACT.Identity, scale=al_col[:, b:b + 1])
+        bank = new_bank("x")
+        for b in range(4):
+            nc.tensor.transpose(bank[:, b, :], scaled[:, b, :], ident[:])
+        nc.scalar.copy(half(t[0], 0), bank[:].rearrange("p b c -> p (b c)"))
+        bank = to_columns(half(q[0], 0), "u0")
+        first_col = keep.tile([P, 4], F32, name="first_col")
+        for b in range(4):
+            nc.scalar.activation(junk[:], bank[:, b, :], ACT.Identity, scale=share_col[:, b:b + 1],
+                                 accum_out=first_col[:, b:b + 1])
+
+        groups = [(0, 4, new_bank("qa")), (4, 2, new_bank("qb")), (6, 2, new_bank("u1"))]
+
+        def add_up(j, c0, n):
+            for g0, blocks, bank in groups:
+                first_j = 1 if g0 == 0 else 0
+                for b in range(blocks):
+                    c = (g0 + b) * P
+                    if c0 <= c < c0 + n:
+                        nc.tensor.matmul(bank[:, b, :], q[j][:, c:c + P], ident[:], is_transpose=True,
+                                         start=(j == first_j and b == 0), stop=(j == BLOCKS - 1 and b == blocks - 1))
+
+        for j0 in range(0, BLOCKS, 2):
             for a in range(2):
-                nc.vector.tensor_tensor(half(t[j], a), u[j][:].indirect(half_list(dst_l, a)), half(al, a), MULT)
-            for a in range(2):
-                nc.vector.tensor_tensor(half(q[j], a), h[j][:].indirect(half_list(src_l, a)), half(t[j], a), MULT)
-                for b in range(4):
-                    c0 = a * HALF + b * P
-                    nc.tensor.matmul(sums[a][:, b, :], q[j][:, c0:c0 + P], ident[:], is_transpose=True,
-                                     start=(j == 0 and b == 0), stop=(j == BLOCKS - 1 and b == 3))
+                pair = [j for j in (j0, j0 + 1) if (j, a) != (0, 0)]
+                for j in pair:
+                    scaled_look_up(t[j], u[j], dst_l, al, a * HALF, HALF)
+                for j in pair:
+                    n = HALF // 2 if (j, a) == (BLOCKS - 1, 1) else HALF
+                    for c0 in range(a * HALF, (a + 1) * HALF, n):
+                        scaled_look_up(q[j], h[j], src_l, t[j], c0, n)
+                        add_up(j, c0, n)
 
         w_col = keep.tile([P, 8], F32, name="w_col")
-        junk = keep.tile([P, P], F32, name="junk")
         w_row = keep.tile([P, EDGES], F32, name="w_row")
-        for a in range(2):
-            for b in range(4):
-                nc.scalar.activation(junk[:], sums[a][:, b, :], ACT.Copy, accum_out=w_col[:, 4 * a + b:4 * a + b + 1])
-            if a == 0:
-                to_row(w_row, w_col, 0, 4, "u0")
+        for g0, blocks, bank in groups:
+            for b in range(blocks):
+                j = g0 + b
+                if g0 == 0:
+                    nc.scalar.activation(junk[:], bank[:, b, :], ACT.Identity, bias=first_col[:, b:b + 1],
+                                         accum_out=w_col[:, j:j + 1])
+                else:
+                    nc.scalar.activation(junk[:], bank[:, b, :], ACT.Copy, accum_out=w_col[:, j:j + 1])
+            if g0 < 6:
+                to_row(w_row, w_col, g0, blocks, "u0" if g0 == 0 else "u2")
             else:
-                to_row(w_row, w_col, 4, 2, "x")
-                to_row(w_row, w_col, 6, 2, "y")
+                to_row(w_row, w_col, 6, 2, "x")
 
         def store_half(j, a, res, queue):
             queue.dma_start(out_0[j * P:(j + 1) * P, a * 256:(a + 1) * 256], res)
 
-        def finish(j, a, to):
-            turned = keep.tile([P, 2, P], F32, name="turned%d%d" % (j, a))
-            nc.scalar.copy(turned[:], pair_columns(to, "xy"[a])[:, :2, :])
-            bank = new_bank("q" + "ab"[a])
-            for b in range(2):
-                nc.tensor.transpose(bank[:, b, :], turned[:, b, :], ident[:])
+        def gp_pair_sum(dst, gathered):
+            nc.gpsimd.tensor_tensor(dst, gathered[:, 0::2], gathered[:, 1::2], ADD)
+
+        def finish(j, a, to, add):
             res = keep.tile([P, 2 * P], F32, name="res%d%d" % (j, a))
-            nc.scalar.copy(res[:], bank[:, :2, :].rearrange("p b c -> p (b c)"))
+            add(res[:], to)
             store_half(j, a, res[:], nc.sync)
 
         def node_halves(pieces, tag):
             to = keep.tile([P, len(pieces) * HALF], F32, name="to", tag=tag)
             for i, (j, a) in enumerate(pieces):
                 look_up(half(to, i), t[j], out_l, a)
-            return to
+                finish(j, a, half(to, i), pair_sum if (j, a) == (3, 1) else gp_pair_sum)
 
-        first = [(0, 0), (0, 1), (1, 0)]
-        to = node_halves(first, "first")
-        for i, (j, a) in enumerate(first):
-            finish(j, a, half(to, i))
+        node_halves([(0, 0), (0, 1), (1, 0)], "first")
         wi = keep.tile([P, EDGES], F32, name="wi")
-        sw_col = keep.tile([P, 4], F32, name="sw_col")
         for a in range(2):
             look_up(half(wi, a), w_row, inn_l, a)
-            nc.scalar.copy(sw_col[:, 2 * a:2 * a + 2], pair_columns(half(wi, a), "u%d" % (1 + a))[:, :2, 0])
-        to_row(sw, sw_col, 0, 2, "u3")
-        to_row(sw, sw_col, 2, 1, "x")
-        to_row(sw, sw_col, 3, 1, "y")
-        second = [(1, 1), (2, 0)]
-        to = node_halves(second, "w_row")
-        for i, (j, a) in enumerate(second):
-            finish(j, a, half(to, i))
+            gp_pair_sum(sw[:, a * 256:(a + 1) * 256], half(wi, a))
+        node_halves([(1, 1)], "w_row")
         sb = keep.tile([P, EDGES], F32, name="sb")
         for a in range(2):
             look_up(half(sb, a), sw, dst_l, a)
@@ -226,10 +253,5 @@ def tile_attend_ggattn_kernel(tc, hT, W, dyT, sc, dstoffs, innoffs, soffs, ooffs
         nc.tensor.transpose(bank[:, 0, :], o1col[:], ident[:])
         o1row = keep.tile([8, P], F32, name="o1row")
         nc.scalar.copy(o1row[:], bank[0:8, 0, :])
-        nc.sync.dma_start(out_1.rearrange("o (j p) -> (o j) p", p=P), o1row[:])
-        to = node_halves([(2, 1), (3, 0), (3, 1)], "sw")
-        finish(2, 1, half(to, 0))
-        res = keep.tile([P, NODES], F32, name="res3")
-        for a in range(2):
-            pair_sum(res[:, a * 256:(a + 1) * 256], half(to, 1 + a))
-            store_half(3, a, res[:, a * 256:(a + 1) * 256], nc.sync)
+        nc.scalar.dma_start(out_1.rearrange("o (j p) -> (o j) p", p=P), o1row[:])
+        node_halves([(2, 0), (2, 1), (3, 0), (3, 1)], "sw")

@@ -63,19 +63,20 @@ def tile_attend_ggattn_kernel(tc, hT, W, dyT, sc, dstoffs, innoffs, soffs, ooffs
 
         sc_row = keep.tile([1, EDGES], F32, name="sc_row", tag="dy_bf", align_bytes=64)
         dy_raw = [keep.tile([P, 4, 256], F32, name="dy_raw%d" % a) for a in range(2)]
-        w_parts = [(0, 1), (1, 1), (2, 2)]
-        w_raw = [keep.tile([P, 4, n * P], F32, name="w_raw%d" % j) for j, n in w_parts]
+        w_raw = [keep.tile([P, 4, 2 * P], F32, name="w_raw%d" % i) for i in range(2)]
         nc.sync.dma_start(sc_row[:], sc[0:1, :])
+        nc.sync.dma_start(src_l[:], soffs)
+        nc.sync.dma_start(h[0][:, :NODES], hT[0:P, :])
         nc.sync.dma_start(inn_l[:], innoffs)
         nc.sync.dma_start(dst_l[:], dstoffs)
         dyv = dyT.rearrange("(p j) x -> p j x", j=4)
         for a in range(2):
             nc.sync.dma_start(dy_raw[a][:], dyv[:, :, a * 256:(a + 1) * 256])
+        nc.sync.dma_start(h[1][:, :NODES], hT[P:2 * P, :])
         Wv = W.rearrange("(p j) d -> p j d", j=4)
-        for i, (j, n) in enumerate(w_parts):
-            nc.sync.dma_start(w_raw[i][:], Wv[:, :, j * P:(j + n) * P])
-        nc.sync.dma_start(src_l[:], soffs)
-        for j in range(BLOCKS):
+        for i in range(2):
+            nc.sync.dma_start(w_raw[i][:], Wv[:, :, i * 2 * P:(i + 1) * 2 * P])
+        for j in range(2, BLOCKS):
             nc.sync.dma_start(h[j][:, :NODES], hT[j * P:(j + 1) * P, :])
         nc.sync.dma_start(out_l[:], ooffs)
 
@@ -97,15 +98,21 @@ def tile_attend_ggattn_kernel(tc, hT, W, dyT, sc, dstoffs, innoffs, soffs, ooffs
         def pair_sum(dst, gathered):
             nc.vector.tensor_tensor(dst, gathered[:, 0::2], gathered[:, 1::2], ADD)
 
+        def gp_pair_sum(dst, gathered):
+            nc.gpsimd.tensor_tensor(dst, gathered[:, 0::2], gathered[:, 1::2], ADD)
+
         def look_up(dst, window, offs, a):
             nc.vector.tensor_copy(dst, window[:].indirect(half_list(offs, a)))
 
         nc.scalar.activation(e[0:1, :], sc_row[:], ACT.Exp)
         e_banks = [to_columns(half(e, a), "q" + "ab"[a]) for a in range(2)]
+        hs = [keep.tile([P, HALF], F32, name="hs%d" % j) for j in range(2)]
+        look_up(hs[0][:], h[0], src_l, 0)
         es = keep.tile([P, EDGES], F32, name="es")
         for a in range(2):
             look_up(half(es, a), e, inn_l, a)
-        pair_sum(den[:, :NODES], es[:])
+            gp_pair_sum(den[:, a * 256:(a + 1) * 256], half(es, a))
+        look_up(hs[1][:], h[1], src_l, 0)
 
         al_col = keep.tile([P, 8], F32, name="al_col")
         nal_col = keep.tile([P, 8], F32, name="nal_col")
@@ -118,111 +125,105 @@ def tile_attend_ggattn_kernel(tc, hT, W, dyT, sc, dstoffs, innoffs, soffs, ooffs
         dy_s = keep.tile([P, NODES], U8, name="dy_s", align_bytes=64)
         nc.vector.quantize_mx(out=dy_q[:].bitcast(E5M2), scales=dy_s[:], in_=dy_bf[:].rearrange("p x j -> p (x j)"))
 
-        def product(j0, n, tag):
-            w_bf = keep.tile([P, n * P, 4], BF16, name="w_bf%d" % j0, tag=tag, align_bytes=64)
-            nc.scalar.copy(w_bf[:], w_raw[j0][:].rearrange("p j d -> p d j"))
-            w_q = keep.tile([P, n * P], U32, name="w_q%d" % j0, align_bytes=64)
-            w_s = keep.tile([P, n * P], U8, name="w_s%d" % j0, align_bytes=64)
+        def products(i):
+            w_bf = keep.tile([P, 2 * P, 4], BF16, name="w_bf%d" % i, align_bytes=64)
+            nc.scalar.copy(w_bf[:], w_raw[i][:].rearrange("p j d -> p d j"))
+            w_q = keep.tile([P, 2 * P], U32, name="w_q%d" % i, align_bytes=64)
+            w_s = keep.tile([P, 2 * P], U8, name="w_s%d" % i, align_bytes=64)
             nc.vector.quantize_mx(out=w_q[:].bitcast(E4M3), scales=w_s[:], in_=w_bf[:].rearrange("p d j -> p (d j)"))
-            for i in range(n):
-                cols = slice(i * P, (i + 1) * P)
-                acc = psum.tile([P, NODES], F32, name="acc", tag="u%d" % (j0 + i))
+            for b in range(2):
+                cols = slice(b * P, (b + 1) * P)
+                acc = psum.tile([P, NODES], F32, name="acc", tag="u%d" % (2 * i + b))
                 nc.tensor.matmul_mx(out=acc[:], lhsT=w_q[:, cols].bitcast(E4M3), lhsT_scale=w_s[:, cols],
                                     rhs=dy_q[:].bitcast(E5M2), rhs_scale=dy_s[:], start=True, stop=True)
-                nc.scalar.copy(u[j0 + i][:, :NODES], acc[:])
+                nc.scalar.copy(u[2 * i + b][:, :NODES], acc[:])
 
-        product(0, 1, "w_bf0")
-        e_col = keep.tile([P, 8], F32, name="e_col", tag="w_raw0")
-        for a in range(2):
-            nc.scalar.copy(e_col[:, 4 * a:4 * a + 4], e_banks[a][:, :, 0])
-        dn0 = keep.tile([P, HALF], F32, name="dn0", tag="w_bf0", align_bytes=64)
-        look_up(dn0[:], den, dst_l, 0)
-        dn1 = keep.tile([P, HALF], F32, name="dn1")
-        look_up(dn1[:], den, dst_l, 1)
-
-        def weights(a, dn, rdn_tag):
+        def weights(a, dn_bank):
             cols = slice(4 * a, 4 * a + 4)
-            rdn = keep.tile([P, 4], F32, name="rdn%d" % a, tag=rdn_tag)
-            nc.vector.reciprocal(rdn[:], to_columns(dn, ("x", "u0")[a])[:, :, 0])
-            nc.vector.tensor_tensor(al_col[:, cols], rdn[:], e_col[:, cols], MULT)
+            rdn = keep.tile([P, 4], F32, name="rdn%d" % a)
+            nc.vector.reciprocal(rdn[:], dn_bank[:, :, 0])
+            nc.vector.tensor_tensor(al_col[:, cols], rdn[:], e_banks[a][:, :, 0], MULT)
             to_row(al, al_col, 4 * a, 4, "yx"[a])
-
-        weights(0, dn0, "den")
 
         t = [keep.tile([P, EDGES], F32, name="t%d" % j) for j in range(BLOCKS)]
         q = [keep.tile([P, EDGES], F32, name="q%d" % j) for j in range(BLOCKS)]
         junk = keep.tile([P, P], F32, name="junk")
 
-        def scaled_look_up(dst, window, offs, other, c0, n):
-            nc.vector.tensor_tensor(dst[:, c0:c0 + n], window[:].indirect(offs[:, c0 // 16:(c0 + n) // 16]),
-                                    other[:, c0:c0 + n], MULT)
-
-        ud = keep.tile([P, HALF], F32, name="ud")
-        product(1, 1, "w_bf1")
-        product(2, 2, "w_bf2")
-        look_up(ud[:], u[0], dst_l, 0)
-        weights(1, dn1, "rdn1")
-        scaled_look_up(q[0], h[0], src_l, ud, 0, HALF)
+        products(0)
+        dn0 = keep.tile([P, HALF], F32, name="dn0", tag="w_bf0", align_bytes=64)
+        look_up(dn0[:], den, dst_l, 0)
+        dn_bank = to_columns(dn0, "x")
+        products(1)
+        ud = [keep.tile([P, HALF], F32, name="ud%d" % j) for j in range(2)]
+        look_up(ud[0][:], u[0], dst_l, 0)
+        nc.gpsimd.tensor_tensor(half(q[0], 0), ud[0][:], hs[0][:], MULT)
+        weights(0, dn_bank)
+        look_up(ud[1][:], u[1], dst_l, 0)
+        nc.gpsimd.tensor_tensor(half(q[1], 0), ud[1][:], hs[1][:], MULT)
+        dn1 = keep.tile([P, HALF], F32, name="dn1", tag="dy_q", align_bytes=64)
+        look_up(dn1[:], den, dst_l, 1)
+        weights(1, to_columns(dn1, "u0"))
         nc.scalar.mul(nal_col[:], al_col[:], -1.0)
         share_col = keep.tile([P, 4], F32, name="share_col")
         nc.scalar.mul(share_col[:], al_col[:, 0:4], 1.0 / P)
 
-        bank = to_columns(ud, "y")
-        scaled = keep.tile([P, 4, P], F32, name="scaled")
+        for j in range(2):
+            bank = to_columns(ud[j], "y")
+            scaled = keep.tile([P, 4, P], F32, name="scaled%d" % j)
+            for b in range(4):
+                nc.scalar.activation(scaled[:, b, :], bank[:, b, :], ACT.Identity, scale=al_col[:, b:b + 1])
+            bank = new_bank("x")
+            for b in range(4):
+                nc.tensor.transpose(bank[:, b, :], scaled[:, b, :], ident[:])
+            nc.scalar.copy(half(t[j], 0), bank[:].rearrange("p b c -> p (b c)"))
+        bank = new_bank("u0")
         for b in range(4):
-            nc.scalar.activation(scaled[:, b, :], bank[:, b, :], ACT.Identity, scale=al_col[:, b:b + 1])
-        bank = new_bank("x")
-        for b in range(4):
-            nc.tensor.transpose(bank[:, b, :], scaled[:, b, :], ident[:])
-        nc.scalar.copy(half(t[0], 0), bank[:].rearrange("p b c -> p (b c)"))
-        bank = to_columns(half(q[0], 0), "u0")
+            for j in range(2):
+                nc.tensor.matmul(bank[:, b, :], q[j][:, b * P:(b + 1) * P], ident[:], is_transpose=True,
+                                 start=(j == 0), stop=(j == 1))
         first_col = keep.tile([P, 4], F32, name="first_col")
         for b in range(4):
             nc.scalar.activation(junk[:], bank[:, b, :], ACT.Identity, scale=share_col[:, b:b + 1],
                                  accum_out=first_col[:, b:b + 1])
 
+        def scaled_look_up(dst, window, offs, other, c0, n):
+            nc.vector.tensor_tensor(dst[:, c0:c0 + n], window[:].indirect(offs[:, c0 // 16:(c0 + n) // 16]),
+                                    other[:, c0:c0 + n], MULT)
+
         groups = [(0, 4, new_bank("qa")), (4, 2, new_bank("qb")), (6, 2, new_bank("u1"))]
+        w_col = keep.tile([P, 8], F32, name="w_col")
+        w_row = keep.tile([P, EDGES], F32, name="w_row")
 
         def add_up(j, c0, n):
             for g0, blocks, bank in groups:
-                first_j = 1 if g0 == 0 else 0
+                if not c0 <= g0 * P < c0 + n:
+                    continue
+                first_j = 2 if g0 == 0 else 0
                 for b in range(blocks):
                     c = (g0 + b) * P
-                    if c0 <= c < c0 + n:
-                        nc.tensor.matmul(bank[:, b, :], q[j][:, c:c + P], ident[:], is_transpose=True,
-                                         start=(j == first_j and b == 0), stop=(j == BLOCKS - 1 and b == blocks - 1))
+                    nc.tensor.matmul(bank[:, b, :], q[j][:, c:c + P], ident[:], is_transpose=True,
+                                     start=(j == first_j and b == 0), stop=(j == BLOCKS - 1 and b == blocks - 1))
+                if j == BLOCKS - 1:
+                    for b in range(blocks):
+                        sums = w_col[:, g0 + b:g0 + b + 1]
+                        if g0 == 0:
+                            nc.scalar.activation(junk[:], bank[:, b, :], ACT.Identity, bias=first_col[:, b:b + 1],
+                                                 accum_out=sums)
+                        else:
+                            nc.scalar.activation(junk[:], bank[:, b, :], ACT.Copy, accum_out=sums)
+                    to_row(w_row, w_col, g0, blocks, {0: "u0", 4: "u2", 6: "x"}[g0])
 
-        for j0 in range(0, BLOCKS, 2):
-            for a in range(2):
-                pair = [j for j in (j0, j0 + 1) if (j, a) != (0, 0)]
-                for j in pair:
-                    scaled_look_up(t[j], u[j], dst_l, al, a * HALF, HALF)
-                for j in pair:
-                    n = HALF // 2 if (j, a) == (BLOCKS - 1, 1) else HALF
-                    for c0 in range(a * HALF, (a + 1) * HALF, n):
-                        scaled_look_up(q[j], h[j], src_l, t[j], c0, n)
-                        add_up(j, c0, n)
-
-        w_col = keep.tile([P, 8], F32, name="w_col")
-        w_row = keep.tile([P, EDGES], F32, name="w_row")
-        for g0, blocks, bank in groups:
-            for b in range(blocks):
-                j = g0 + b
-                if g0 == 0:
-                    nc.scalar.activation(junk[:], bank[:, b, :], ACT.Identity, bias=first_col[:, b:b + 1],
-                                         accum_out=w_col[:, j:j + 1])
-                else:
-                    nc.scalar.activation(junk[:], bank[:, b, :], ACT.Copy, accum_out=w_col[:, j:j + 1])
-            if g0 < 6:
-                to_row(w_row, w_col, g0, blocks, "u0" if g0 == 0 else "u2")
-            else:
-                to_row(w_row, w_col, 6, 2, "x")
+        for a, js in ((0, (2, 3)), (1, (0, 1)), (1, (2, 3))):
+            for j in js:
+                scaled_look_up(t[j], u[j], dst_l, al, a * HALF, HALF)
+            n = HALF // 2 if (js[0], a) == (2, 1) else HALF
+            for c0 in range(a * HALF, (a + 1) * HALF, n):
+                for j in js:
+                    scaled_look_up(q[j], h[j], src_l, t[j], c0, n)
+                    add_up(j, c0, n)
 
         def store_half(j, a, res, queue):
             queue.dma_start(out_0[j * P:(j + 1) * P, a * 256:(a + 1) * 256], res)
-
-        def gp_pair_sum(dst, gathered):
-            nc.gpsimd.tensor_tensor(dst, gathered[:, 0::2], gathered[:, 1::2], ADD)
 
         def finish(j, a, to, add):
             res = keep.tile([P, 2 * P], F32, name="res%d%d" % (j, a))
@@ -240,7 +241,7 @@ def tile_attend_ggattn_kernel(tc, hT, W, dyT, sc, dstoffs, innoffs, soffs, ooffs
         for a in range(2):
             look_up(half(wi, a), w_row, inn_l, a)
             gp_pair_sum(sw[:, a * 256:(a + 1) * 256], half(wi, a))
-        node_halves([(1, 1)], "w_row")
+        node_halves([(1, 1), (2, 0)], "w_row")
         sb = keep.tile([P, EDGES], F32, name="sb")
         for a in range(2):
             look_up(half(sb, a), sw, dst_l, a)
@@ -254,4 +255,4 @@ def tile_attend_ggattn_kernel(tc, hT, W, dyT, sc, dstoffs, innoffs, soffs, ooffs
         o1row = keep.tile([8, P], F32, name="o1row")
         nc.scalar.copy(o1row[:], bank[0:8, 0, :])
         nc.scalar.dma_start(out_1.rearrange("o (j p) -> (o j) p", p=P), o1row[:])
-        node_halves([(2, 0), (2, 1), (3, 0), (3, 1)], "sw")
+        node_halves([(2, 1), (3, 0), (3, 1)], "sw")

@@ -64,20 +64,20 @@ def tile_attend_ggattn_kernel(tc, hT, W, dyT, sc, dstoffs, innoffs, soffs, ooffs
         sc_row = keep.tile([1, EDGES], F32, name="sc_row", tag="dy_bf", align_bytes=64)
         dy_raw = [keep.tile([P, 4, 256], F32, name="dy_raw%d" % a) for a in range(2)]
         w_raw = [keep.tile([P, 4, 2 * P], F32, name="w_raw%d" % i) for i in range(2)]
-        nc.sync.dma_start(sc_row[:], sc[0:1, :])
         nc.sync.dma_start(src_l[:], soffs)
         nc.sync.dma_start(h[0][:, :NODES], hT[0:P, :])
+        nc.sync.dma_start(sc_row[:], sc[0:1, :])
+        nc.sync.dma_start(h[1][:, :NODES], hT[P:2 * P, :])
         nc.sync.dma_start(inn_l[:], innoffs)
         nc.sync.dma_start(dst_l[:], dstoffs)
         dyv = dyT.rearrange("(p j) x -> p j x", j=4)
         for a in range(2):
             nc.sync.dma_start(dy_raw[a][:], dyv[:, :, a * 256:(a + 1) * 256])
-        nc.sync.dma_start(h[1][:, :NODES], hT[P:2 * P, :])
+        nc.sync.dma_start(h[2][:, :NODES], hT[2 * P:3 * P, :])
         Wv = W.rearrange("(p j) d -> p j d", j=4)
         for i in range(2):
             nc.sync.dma_start(w_raw[i][:], Wv[:, :, i * 2 * P:(i + 1) * 2 * P])
-        for j in range(2, BLOCKS):
-            nc.sync.dma_start(h[j][:, :NODES], hT[j * P:(j + 1) * P, :])
+        nc.sync.dma_start(h[3][:, :NODES], hT[3 * P:, :])
         nc.sync.dma_start(out_l[:], ooffs)
 
         def new_bank(tag):
@@ -106,13 +106,14 @@ def tile_attend_ggattn_kernel(tc, hT, W, dyT, sc, dstoffs, innoffs, soffs, ooffs
 
         nc.scalar.activation(e[0:1, :], sc_row[:], ACT.Exp)
         e_banks = [to_columns(half(e, a), "q" + "ab"[a]) for a in range(2)]
-        hs = [keep.tile([P, HALF], F32, name="hs%d" % j) for j in range(2)]
-        look_up(hs[0][:], h[0], src_l, 0)
+        hs = [keep.tile([P, HALF], F32, name="hs%d" % j) for j in range(3)]
+        for j in range(2):
+            look_up(hs[j][:], h[j], src_l, 0)
         es = keep.tile([P, EDGES], F32, name="es")
         for a in range(2):
             look_up(half(es, a), e, inn_l, a)
             gp_pair_sum(den[:, a * 256:(a + 1) * 256], half(es, a))
-        look_up(hs[1][:], h[1], src_l, 0)
+        look_up(hs[2][:], h[2], src_l, 0)
 
         al_col = keep.tile([P, 8], F32, name="al_col")
         nal_col = keep.tile([P, 8], F32, name="nal_col")
@@ -139,56 +140,33 @@ def tile_attend_ggattn_kernel(tc, hT, W, dyT, sc, dstoffs, innoffs, soffs, ooffs
                 nc.scalar.copy(u[2 * i + b][:, :NODES], acc[:])
 
         def weights(a, dn_bank):
-            cols = slice(4 * a, 4 * a + 4)
             rdn = keep.tile([P, 4], F32, name="rdn%d" % a)
             nc.vector.reciprocal(rdn[:], dn_bank[:, :, 0])
-            nc.vector.tensor_tensor(al_col[:, cols], rdn[:], e_banks[a][:, :, 0], MULT)
-            to_row(al, al_col, 4 * a, 4, "yx"[a])
+            for b in range(4):
+                nc.scalar.activation(al_col[:, 4 * a + b:4 * a + b + 1], e_banks[a][:, b, 0:1], ACT.Identity,
+                                     scale=rdn[:, b:b + 1])
 
         t = [keep.tile([P, EDGES], F32, name="t%d" % j) for j in range(BLOCKS)]
         q = [keep.tile([P, EDGES], F32, name="q%d" % j) for j in range(BLOCKS)]
         junk = keep.tile([P, P], F32, name="junk")
 
-        products(0)
-        dn0 = keep.tile([P, HALF], F32, name="dn0", tag="w_bf0", align_bytes=64)
-        look_up(dn0[:], den, dst_l, 0)
-        dn_bank = to_columns(dn0, "x")
-        products(1)
-        ud = [keep.tile([P, HALF], F32, name="ud%d" % j) for j in range(2)]
-        look_up(ud[0][:], u[0], dst_l, 0)
-        nc.gpsimd.tensor_tensor(half(q[0], 0), ud[0][:], hs[0][:], MULT)
-        weights(0, dn_bank)
-        look_up(ud[1][:], u[1], dst_l, 0)
-        nc.gpsimd.tensor_tensor(half(q[1], 0), ud[1][:], hs[1][:], MULT)
-        dn1 = keep.tile([P, HALF], F32, name="dn1", tag="dy_q", align_bytes=64)
-        look_up(dn1[:], den, dst_l, 1)
-        weights(1, to_columns(dn1, "u0"))
-        nc.scalar.mul(nal_col[:], al_col[:], -1.0)
-        share_col = keep.tile([P, 4], F32, name="share_col")
-        nc.scalar.mul(share_col[:], al_col[:, 0:4], 1.0 / P)
-
-        for j in range(2):
-            bank = to_columns(ud[j], "y")
-            scaled = keep.tile([P, 4, P], F32, name="scaled%d" % j)
-            for b in range(4):
-                nc.scalar.activation(scaled[:, b, :], bank[:, b, :], ACT.Identity, scale=al_col[:, b:b + 1])
-            bank = new_bank("x")
-            for b in range(4):
-                nc.tensor.transpose(bank[:, b, :], scaled[:, b, :], ident[:])
-            nc.scalar.copy(half(t[j], 0), bank[:].rearrange("p b c -> p (b c)"))
-        bank = new_bank("u0")
-        for b in range(4):
-            for j in range(2):
-                nc.tensor.matmul(bank[:, b, :], q[j][:, b * P:(b + 1) * P], ident[:], is_transpose=True,
-                                 start=(j == 0), stop=(j == 1))
-        first_col = keep.tile([P, 4], F32, name="first_col")
-        for b in range(4):
-            nc.scalar.activation(junk[:], bank[:, b, :], ACT.Identity, scale=share_col[:, b:b + 1],
-                                 accum_out=first_col[:, b:b + 1])
-
         def scaled_look_up(dst, window, offs, other, c0, n):
-            nc.vector.tensor_tensor(dst[:, c0:c0 + n], window[:].indirect(offs[:, c0 // 16:(c0 + n) // 16]),
-                                    other[:, c0:c0 + n], MULT)
+            nc.vector.tensor_tensor(dst, window[:].indirect(offs[:, c0 // 16:(c0 + n) // 16]), other, MULT)
+
+        products(0)
+        dn = keep.tile([P, EDGES], F32, name="dn", tag="w_bf0", align_bytes=64)
+        for a in range(2):
+            look_up(half(dn, a), den, dst_l, a)
+        products(1)
+        ud = [keep.tile([P, HALF], F32, name="ud%d" % j) for j in range(BLOCKS)]
+        for j in range(BLOCKS):
+            look_up(ud[j][:], u[j], dst_l, 0)
+            if j < 3:
+                nc.gpsimd.tensor_tensor(half(q[j], 0), ud[j][:], hs[j][:], MULT)
+        for a in range(2):
+            weights(a, to_columns(half(dn, a), "xy"[a]))
+        to_row(al, al_col, 4, 4, "u0")
+        nc.scalar.mul(nal_col[:], al_col[:], -1.0)
 
         groups = [(0, 4, new_bank("qa")), (4, 2, new_bank("qb")), (6, 2, new_bank("u1"))]
         w_col = keep.tile([P, 8], F32, name="w_col")
@@ -198,43 +176,55 @@ def tile_attend_ggattn_kernel(tc, hT, W, dyT, sc, dstoffs, innoffs, soffs, ooffs
             for g0, blocks, bank in groups:
                 if not c0 <= g0 * P < c0 + n:
                     continue
-                first_j = 2 if g0 == 0 else 0
                 for b in range(blocks):
                     c = (g0 + b) * P
                     nc.tensor.matmul(bank[:, b, :], q[j][:, c:c + P], ident[:], is_transpose=True,
-                                     start=(j == first_j and b == 0), stop=(j == BLOCKS - 1 and b == blocks - 1))
+                                     start=(j == 0 and b == 0), stop=(j == BLOCKS - 1 and b == blocks - 1))
                 if j == BLOCKS - 1:
                     for b in range(blocks):
                         sums = w_col[:, g0 + b:g0 + b + 1]
                         if g0 == 0:
-                            nc.scalar.activation(junk[:], bank[:, b, :], ACT.Identity, bias=first_col[:, b:b + 1],
+                            nc.scalar.activation(junk[:], bank[:, b, :], ACT.Identity, scale=al_col[:, b:b + 1],
                                                  accum_out=sums)
                         else:
                             nc.scalar.activation(junk[:], bank[:, b, :], ACT.Copy, accum_out=sums)
                     to_row(w_row, w_col, g0, blocks, {0: "u0", 4: "u2", 6: "x"}[g0])
 
-        for a, js in ((0, (2, 3)), (1, (0, 1)), (1, (2, 3))):
+        for j in range(BLOCKS):
+            if j == 3:
+                scaled_look_up(half(q[j], 0), h[j], src_l, ud[j][:], 0, HALF)
+            add_up(j, 0, HALF)
+
+        for j in range(BLOCKS):
+            bank = to_columns(ud[j], "xy"[j % 2])
+            scaled = keep.tile([P, 4, P], F32, name="scaled%d" % j)
+            for b in range(4):
+                nc.scalar.activation(scaled[:, b, :], bank[:, b, :], ACT.Identity, scale=al_col[:, b:b + 1])
+            bank = new_bank("u%d" % (2 + j % 2))
+            for b in range(4):
+                nc.tensor.transpose(bank[:, b, :], scaled[:, b, :], ident[:])
+            nc.scalar.copy(half(t[j], 0), bank[:].rearrange("p b c -> p (b c)"))
+
+        for js, n in (((0, 1), HALF), ((2, 3), HALF // 2)):
             for j in js:
-                scaled_look_up(t[j], u[j], dst_l, al, a * HALF, HALF)
-            n = HALF // 2 if (js[0], a) == (2, 1) else HALF
-            for c0 in range(a * HALF, (a + 1) * HALF, n):
+                scaled_look_up(half(t[j], 1), u[j], dst_l, half(al, 1), HALF, HALF)
+            for c0 in range(HALF, EDGES, n):
                 for j in js:
-                    scaled_look_up(q[j], h[j], src_l, t[j], c0, n)
+                    scaled_look_up(q[j][:, c0:c0 + n], h[j], src_l, t[j][:, c0:c0 + n], c0, n)
                     add_up(j, c0, n)
-
-        def store_half(j, a, res, queue):
-            queue.dma_start(out_0[j * P:(j + 1) * P, a * 256:(a + 1) * 256], res)
-
-        def finish(j, a, to, add):
-            res = keep.tile([P, 2 * P], F32, name="res%d%d" % (j, a))
-            add(res[:], to)
-            store_half(j, a, res[:], nc.sync)
 
         def node_halves(pieces, tag):
             to = keep.tile([P, len(pieces) * HALF], F32, name="to", tag=tag)
             for i, (j, a) in enumerate(pieces):
-                look_up(half(to, i), t[j], out_l, a)
-                finish(j, a, half(to, i), pair_sum if (j, a) == (3, 1) else gp_pair_sum)
+                n = HALF // 2 if (j, a) == (BLOCKS - 1, 1) else HALF
+                for c0 in range(0, HALF, n):
+                    part = to[:, i * HALF + c0:i * HALF + c0 + n]
+                    first = a * HALF + c0
+                    nc.vector.tensor_copy(part, t[j][:].indirect(out_l[:, first // 16:(first + n) // 16]))
+                    res = keep.tile([P, n // 2], F32, name="res%d_%d" % (j, first))
+                    last = j == BLOCKS - 1 and first + n == EDGES
+                    (pair_sum if last else gp_pair_sum)(res[:], part)
+                    nc.sync.dma_start(out_0[j * P:(j + 1) * P, first // 2:(first + n) // 2], res[:])
 
         node_halves([(0, 0), (0, 1), (1, 0)], "first")
         wi = keep.tile([P, EDGES], F32, name="wi")

@@ -15,10 +15,16 @@ MULT = mybir.AluOpType.mult
 ADD = mybir.AluOpType.add
 
 P = 128
+PACK = 4
 NODES = 512
 EDGES = 1024
 HALF = EDGES // 2
+HALF_NODES = NODES // 2
 BLOCKS = 4
+LAST = BLOCKS - 1
+GROUPS = EDGES // P
+PER_BANK = 4
+PER_COLUMN = 16
 SPARE = 8
 FLOPS = 2 * 512 * 512 * 512
 
@@ -29,26 +35,50 @@ def tile_attend_ggattn_kernel(tc, hT, W, dyT, sc, dstoffs, innoffs, soffs, ooffs
         keep = ctx.enter_context(tc.tile_pool(name="keep", bufs=1))
         psum = ctx.enter_context(tc.psum_pool(name="psum", bufs=1))
 
-        def half_list(offs, a):
-            return offs[:, a * (HALF // 16):(a + 1) * (HALF // 16)]
+        def half(tile, a):
+            return tile[:, a * HALF:(a + 1) * HALF]
 
-        def half(t, a):
-            return t[:, a * HALF:(a + 1) * HALF]
+        def entries(offsets, first, count):
+            return offsets[:, first // PER_COLUMN:(first + count) // PER_COLUMN]
 
         def node_window(name):
-            t = keep.tile([P, NODES + SPARE], F32, name=name)
-            nc.vector.memset(t[:, NODES:], 0.0)
-            return t
+            window = keep.tile([P, NODES + SPARE], F32, name=name)
+            nc.vector.memset(window[:, NODES:], 0.0)
+            return window
 
-        src_l = keep.tile([P, EDGES // 16], U16, name="src_l")
-        inn_l = keep.tile([P, EDGES // 16], U16, name="inn_l")
-        dst_l = keep.tile([P, EDGES // 16], U16, name="dst_l")
-        out_l = keep.tile([P, EDGES // 16], U16, name="out_l")
+        def new_bank(tag):
+            return psum.tile([P, PER_BANK, P], F32, name="bank", tag=tag)
 
-        warm = keep.tile([P, 8], F32, name="warm")
-        nc.vector.memset(warm[:], 0.0)
-        warm2 = keep.tile([P, 8], F32, name="warm2")
-        nc.scalar.activation(warm2[:], warm[:], ACT.Exp)
+        def turn(src, tag):
+            bank = new_bank(tag)
+            for b in range(PER_BANK):
+                nc.tensor.transpose(bank[:, b, :], src[:, b * P:(b + 1) * P], ident[:])
+            return bank
+
+        def to_row(row, columns, k0, count, tag):
+            bank = new_bank(tag)
+            for b in range(count):
+                nc.tensor.transpose(bank[:, b, :], columns[:, k0 + b:k0 + b + 1].to_broadcast([P, P]), ident[:])
+            nc.scalar.copy(row[:, k0 * P:(k0 + count) * P], bank[:, :count, :].rearrange("p b c -> p (b c)"))
+
+        def pair_sum(engine, dst, gathered):
+            engine.tensor_tensor(dst, gathered[:, 0::2], gathered[:, 1::2], ADD)
+
+        def look_up(dst, window, offsets, first, count=HALF):
+            nc.vector.tensor_copy(dst, window[:].indirect(entries(offsets, first, count)))
+
+        def look_up_times(dst, window, offsets, first, count, factor):
+            nc.vector.tensor_tensor(dst, window[:].indirect(entries(offsets, first, count)), factor, MULT)
+
+        src_l = keep.tile([P, EDGES // PER_COLUMN], U16, name="src_l")
+        inn_l = keep.tile([P, EDGES // PER_COLUMN], U16, name="inn_l")
+        dst_l = keep.tile([P, EDGES // PER_COLUMN], U16, name="dst_l")
+        out_l = keep.tile([P, EDGES // PER_COLUMN], U16, name="out_l")
+
+        o1_col = keep.tile([P, P], F32, name="o1_col")
+        filler = (P - GROUPS) // 2
+        nc.vector.memset(o1_col[:, GROUPS:GROUPS + filler], 0.0)
+        nc.scalar.activation(o1_col[:, GROUPS + filler:], o1_col[:, GROUPS:GROUPS + filler], ACT.Exp)
 
         e = keep.tile([P, EDGES], F32, name="e")
         nc.vector.memset(e[:], 0.0)
@@ -58,191 +88,169 @@ def tile_attend_ggattn_kernel(tc, hT, W, dyT, sc, dstoffs, innoffs, soffs, ooffs
         sw = node_window("sw")
         ident = keep.tile([P, P], F32, name="ident")
         make_identity(nc, ident[:])
-        o1col = keep.tile([P, P], F32, name="o1col")
-        nc.gpsimd.memset(o1col[:], 0.0)
 
         sc_row = keep.tile([1, EDGES], F32, name="sc_row", tag="dy_bf", align_bytes=64)
-        dy_raw = [keep.tile([P, 4, 256], F32, name="dy_raw%d" % a) for a in range(2)]
-        w_raw = [keep.tile([P, 4, 2 * P], F32, name="w_raw%d" % i) for i in range(2)]
+        dy_raw = [keep.tile([P, PACK, HALF_NODES], F32, name="dy_raw%d" % a) for a in range(2)]
+        w_raw = [keep.tile([P, PACK, 2 * P], F32, name="w_raw%d" % i) for i in range(2)]
         nc.sync.dma_start(src_l[:], soffs)
-        nc.sync.dma_start(h[0][:, :NODES], hT[0:P, :])
+        nc.scalar.dma_start(h[0][:, :NODES], hT[0:P, :])
         nc.sync.dma_start(sc_row[:], sc[0:1, :])
         nc.sync.dma_start(h[1][:, :NODES], hT[P:2 * P, :])
         nc.sync.dma_start(inn_l[:], innoffs)
         nc.sync.dma_start(dst_l[:], dstoffs)
-        dyv = dyT.rearrange("(p j) x -> p j x", j=4)
+        dy_rows = dyT.rearrange("(p r) x -> p r x", r=PACK)
         for a in range(2):
-            nc.sync.dma_start(dy_raw[a][:], dyv[:, :, a * 256:(a + 1) * 256])
+            nc.sync.dma_start(dy_raw[a][:], dy_rows[:, :, a * HALF_NODES:(a + 1) * HALF_NODES])
         nc.sync.dma_start(h[2][:, :NODES], hT[2 * P:3 * P, :])
-        Wv = W.rearrange("(p j) d -> p j d", j=4)
+        w_rows = W.rearrange("(p r) d -> p r d", r=PACK)
         for i in range(2):
-            nc.sync.dma_start(w_raw[i][:], Wv[:, :, i * 2 * P:(i + 1) * 2 * P])
-        nc.sync.dma_start(h[3][:, :NODES], hT[3 * P:, :])
+            nc.sync.dma_start(w_raw[i][:], w_rows[:, :, i * 2 * P:(i + 1) * 2 * P])
+        nc.sync.dma_start(h[LAST][:, :NODES], hT[LAST * P:, :])
         nc.sync.dma_start(out_l[:], ooffs)
 
-        def new_bank(tag):
-            return psum.tile([P, 4, P], F32, name="bank", tag=tag)
-
-        def to_columns(row, tag):
-            bank = new_bank(tag)
-            for b in range(4):
-                nc.tensor.transpose(bank[:, b, :], row[:, b * P:(b + 1) * P], ident[:])
-            return bank
-
-        def to_row(row, col, j0, n, tag):
-            bank = new_bank(tag)
-            for b in range(n):
-                nc.tensor.transpose(bank[:, b, :], col[:, j0 + b:j0 + b + 1].to_broadcast([P, P]), ident[:])
-            nc.scalar.copy(row[:, j0 * P:(j0 + n) * P], bank[:, :n, :].rearrange("p b c -> p (b c)"))
-
-        def pair_sum(dst, gathered):
-            nc.vector.tensor_tensor(dst, gathered[:, 0::2], gathered[:, 1::2], ADD)
-
-        def gp_pair_sum(dst, gathered):
-            nc.gpsimd.tensor_tensor(dst, gathered[:, 0::2], gathered[:, 1::2], ADD)
-
-        def look_up(dst, window, offs, a):
-            nc.vector.tensor_copy(dst, window[:].indirect(half_list(offs, a)))
-
         nc.scalar.activation(e[0:1, :], sc_row[:], ACT.Exp)
-        e_banks = [to_columns(half(e, a), "q" + "ab"[a]) for a in range(2)]
-        hs = [keep.tile([P, HALF], F32, name="hs%d" % j) for j in range(3)]
+        e_banks = [turn(half(e, a), ("qa", "qb")[a]) for a in range(2)]
+        hs = [keep.tile([P, HALF], F32, name="hs%d" % j) for j in range(LAST)]
         for j in range(2):
             look_up(hs[j][:], h[j], src_l, 0)
         es = keep.tile([P, EDGES], F32, name="es")
         for a in range(2):
-            look_up(half(es, a), e, inn_l, a)
-            gp_pair_sum(den[:, a * 256:(a + 1) * 256], half(es, a))
+            look_up(half(es, a), e, inn_l, a * HALF)
+            pair_sum(nc.gpsimd, den[:, a * HALF_NODES:(a + 1) * HALF_NODES], half(es, a))
         look_up(hs[2][:], h[2], src_l, 0)
 
-        al_col = keep.tile([P, 8], F32, name="al_col")
-        nal_col = keep.tile([P, 8], F32, name="nal_col")
+        al_col = keep.tile([P, GROUPS], F32, name="al_col")
+        minus_al_col = keep.tile([P, GROUPS], F32, name="minus_al_col")
         al = keep.tile([P, EDGES], F32, name="al")
 
-        dy_bf = keep.tile([P, NODES, 4], BF16, name="dy_bf", align_bytes=64)
+        dy_bf = keep.tile([P, NODES, PACK], BF16, name="dy_bf", align_bytes=64)
         for a in range(2):
-            nc.scalar.copy(dy_bf[:, a * 256:(a + 1) * 256, :], dy_raw[a][:].rearrange("p j x -> p x j"))
+            nc.scalar.copy(dy_bf[:, a * HALF_NODES:(a + 1) * HALF_NODES, :], dy_raw[a][:].rearrange("p r x -> p x r"))
         dy_q = keep.tile([P, NODES], U32, name="dy_q", align_bytes=64)
         dy_s = keep.tile([P, NODES], U8, name="dy_s", align_bytes=64)
-        nc.vector.quantize_mx(out=dy_q[:].bitcast(E5M2), scales=dy_s[:], in_=dy_bf[:].rearrange("p x j -> p (x j)"))
+        nc.vector.quantize_mx(out=dy_q[:].bitcast(E5M2), scales=dy_s[:], in_=dy_bf[:].rearrange("p x r -> p (x r)"))
 
         def products(i):
-            w_bf = keep.tile([P, 2 * P, 4], BF16, name="w_bf%d" % i, align_bytes=64)
-            nc.scalar.copy(w_bf[:], w_raw[i][:].rearrange("p j d -> p d j"))
+            w_bf = keep.tile([P, 2 * P, PACK], BF16, name="w_bf%d" % i, align_bytes=64)
+            nc.scalar.copy(w_bf[:], w_raw[i][:].rearrange("p r d -> p d r"))
             w_q = keep.tile([P, 2 * P], U32, name="w_q%d" % i, align_bytes=64)
             w_s = keep.tile([P, 2 * P], U8, name="w_s%d" % i, align_bytes=64)
-            nc.vector.quantize_mx(out=w_q[:].bitcast(E4M3), scales=w_s[:], in_=w_bf[:].rearrange("p d j -> p (d j)"))
+            nc.vector.quantize_mx(out=w_q[:].bitcast(E4M3), scales=w_s[:], in_=w_bf[:].rearrange("p d r -> p (d r)"))
             for b in range(2):
-                cols = slice(b * P, (b + 1) * P)
+                features = slice(b * P, (b + 1) * P)
                 acc = psum.tile([P, NODES], F32, name="acc", tag="u%d" % (2 * i + b))
-                nc.tensor.matmul_mx(out=acc[:], lhsT=w_q[:, cols].bitcast(E4M3), lhsT_scale=w_s[:, cols],
+                nc.tensor.matmul_mx(out=acc[:], lhsT=w_q[:, features].bitcast(E4M3), lhsT_scale=w_s[:, features],
                                     rhs=dy_q[:].bitcast(E5M2), rhs_scale=dy_s[:], start=True, stop=True)
                 nc.scalar.copy(u[2 * i + b][:, :NODES], acc[:])
 
-        def weights(a, dn_bank):
-            rdn = keep.tile([P, 4], F32, name="rdn%d" % a)
-            nc.vector.reciprocal(rdn[:], dn_bank[:, :, 0])
-            for b in range(4):
-                nc.scalar.activation(al_col[:, 4 * a + b:4 * a + b + 1], e_banks[a][:, b, 0:1], ACT.Identity,
-                                     scale=rdn[:, b:b + 1])
-
         t = [keep.tile([P, EDGES], F32, name="t%d" % j) for j in range(BLOCKS)]
         q = [keep.tile([P, EDGES], F32, name="q%d" % j) for j in range(BLOCKS)]
-        junk = keep.tile([P, P], F32, name="junk")
-
-        def scaled_look_up(dst, window, offs, other, c0, n):
-            nc.vector.tensor_tensor(dst, window[:].indirect(offs[:, c0 // 16:(c0 + n) // 16]), other, MULT)
+        sum_out = keep.tile([P, P], F32, name="sum_out")
 
         products(0)
         dn = keep.tile([P, EDGES], F32, name="dn", tag="w_bf0", align_bytes=64)
         for a in range(2):
-            look_up(half(dn, a), den, dst_l, a)
+            look_up(half(dn, a), den, dst_l, a * HALF)
+        for a in range(2):
+            dn_bank = turn(half(dn, a), "xy"[a])
+            dn_inverse = keep.tile([P, PER_BANK], F32, name="dn_inverse%d" % a)
+            nc.vector.reciprocal(dn_inverse[:], dn_bank[:, :, 0])
+            for b in range(PER_BANK):
+                k = PER_BANK * a + b
+                nc.scalar.activation(al_col[:, k:k + 1], e_banks[a][:, b, 0:1], ACT.Identity,
+                                     scale=dn_inverse[:, b:b + 1])
+        to_row(al, al_col, PER_BANK, PER_BANK, "u0")
+        nc.scalar.mul(minus_al_col[:], al_col[:], -1.0)
         products(1)
+
         ud = [keep.tile([P, HALF], F32, name="ud%d" % j) for j in range(BLOCKS)]
         for j in range(BLOCKS):
             look_up(ud[j][:], u[j], dst_l, 0)
-            if j < 3:
+            if j < LAST:
                 nc.gpsimd.tensor_tensor(half(q[j], 0), ud[j][:], hs[j][:], MULT)
-        for a in range(2):
-            weights(a, to_columns(half(dn, a), "xy"[a]))
-        to_row(al, al_col, 4, 4, "u0")
-        nc.scalar.mul(nal_col[:], al_col[:], -1.0)
 
-        groups = [(0, 4, new_bank("qa")), (4, 2, new_bank("qb")), (6, 2, new_bank("u1"))]
-        w_col = keep.tile([P, 8], F32, name="w_col")
+        parts = [(0, 4, new_bank("qa"), "u0"), (4, 2, new_bank("qb"), "u2"), (6, 2, new_bank("u1"), "x")]
+        w_col = keep.tile([P, GROUPS], F32, name="w_col")
         w_row = keep.tile([P, EDGES], F32, name="w_row")
 
-        def add_up(j, c0, n):
-            for g0, blocks, bank in groups:
-                if not c0 <= g0 * P < c0 + n:
+        def add_up(j, first, count):
+            for k0, groups, bank, row_tag in parts:
+                if not first <= k0 * P < first + count:
                     continue
-                for b in range(blocks):
-                    c = (g0 + b) * P
-                    nc.tensor.matmul(bank[:, b, :], q[j][:, c:c + P], ident[:], is_transpose=True,
-                                     start=(j == 0 and b == 0), stop=(j == BLOCKS - 1 and b == blocks - 1))
-                if j == BLOCKS - 1:
-                    for b in range(blocks):
-                        sums = w_col[:, g0 + b:g0 + b + 1]
-                        if g0 == 0:
-                            nc.scalar.activation(junk[:], bank[:, b, :], ACT.Identity, scale=al_col[:, b:b + 1],
-                                                 accum_out=sums)
+                for b in range(groups):
+                    c0 = (k0 + b) * P
+                    nc.tensor.matmul(bank[:, b, :], q[j][:, c0:c0 + P], ident[:], is_transpose=True,
+                                     start=(j == 0 and b == 0), stop=(j == LAST and b == groups - 1))
+                if j == LAST:
+                    for b in range(groups):
+                        k = k0 + b
+                        if k0 * P < HALF:
+                            nc.scalar.activation(sum_out[:], bank[:, b, :], ACT.Identity, scale=al_col[:, k:k + 1],
+                                                 accum_out=w_col[:, k:k + 1])
                         else:
-                            nc.scalar.activation(junk[:], bank[:, b, :], ACT.Copy, accum_out=sums)
-                    to_row(w_row, w_col, g0, blocks, {0: "u0", 4: "u2", 6: "x"}[g0])
+                            nc.scalar.activation(sum_out[:], bank[:, b, :], ACT.Copy, accum_out=w_col[:, k:k + 1])
+                    to_row(w_row, w_col, k0, groups, row_tag)
 
         for j in range(BLOCKS):
-            if j == 3:
-                scaled_look_up(half(q[j], 0), h[j], src_l, ud[j][:], 0, HALF)
+            if j == LAST:
+                look_up_times(half(q[j], 0), h[j], src_l, 0, HALF, ud[j][:])
             add_up(j, 0, HALF)
 
-        for j in range(BLOCKS):
-            bank = to_columns(ud[j], "xy"[j % 2])
-            scaled = keep.tile([P, 4, P], F32, name="scaled%d" % j)
-            for b in range(4):
+        def scale_turned(j, tag):
+            bank = turn(ud[j], tag)
+            scaled = keep.tile([P, PER_BANK, P], F32, name="scaled%d" % j)
+            for b in range(PER_BANK):
                 nc.scalar.activation(scaled[:, b, :], bank[:, b, :], ACT.Identity, scale=al_col[:, b:b + 1])
-            bank = new_bank("u%d" % (2 + j % 2))
-            for b in range(4):
-                nc.tensor.transpose(bank[:, b, :], scaled[:, b, :], ident[:])
-            nc.scalar.copy(half(t[j], 0), bank[:].rearrange("p b c -> p (b c)"))
+            back = new_bank("u%d" % (2 + j % 2))
+            for b in range(PER_BANK):
+                nc.tensor.transpose(back[:, b, :], scaled[:, b, :], ident[:])
+            nc.scalar.copy(half(t[j], 0), back[:].rearrange("p b c -> p (b c)"))
 
-        for js, n in (((0, 1), HALF), ((2, 3), HALF // 2)):
-            for j in js:
-                scaled_look_up(half(t[j], 1), u[j], dst_l, half(al, 1), HALF, HALF)
-            for c0 in range(HALF, EDGES, n):
-                for j in js:
-                    scaled_look_up(q[j][:, c0:c0 + n], h[j], src_l, t[j][:, c0:c0 + n], c0, n)
-                    add_up(j, c0, n)
+        for j in range(2):
+            scale_turned(j, "xy"[j])
 
-        def node_halves(pieces, tag):
+        for pair, count in (((0, 1), HALF), ((2, 3), HALF // 2)):
+            for j in pair:
+                look_up_times(half(t[j], 1), u[j], dst_l, HALF, HALF, half(al, 1))
+            for first in range(HALF, EDGES, count):
+                for j in pair:
+                    edges = slice(first, first + count)
+                    look_up_times(q[j][:, edges], h[j], src_l, first, count, t[j][:, edges])
+                    add_up(j, first, count)
+
+        for j in range(2, BLOCKS):
+            scale_turned(j, "x")
+
+        def node_gradients(pieces, tag):
             to = keep.tile([P, len(pieces) * HALF], F32, name="to", tag=tag)
             for i, (j, a) in enumerate(pieces):
-                n = HALF // 2 if (j, a) == (BLOCKS - 1, 1) else HALF
-                for c0 in range(0, HALF, n):
-                    part = to[:, i * HALF + c0:i * HALF + c0 + n]
+                count = HALF // 2 if (j, a) == (LAST, 1) else HALF
+                for c0 in range(0, HALF, count):
+                    gathered = to[:, i * HALF + c0:i * HALF + c0 + count]
                     first = a * HALF + c0
-                    nc.vector.tensor_copy(part, t[j][:].indirect(out_l[:, first // 16:(first + n) // 16]))
-                    res = keep.tile([P, n // 2], F32, name="res%d_%d" % (j, first))
-                    last = j == BLOCKS - 1 and first + n == EDGES
-                    (pair_sum if last else gp_pair_sum)(res[:], part)
-                    nc.sync.dma_start(out_0[j * P:(j + 1) * P, first // 2:(first + n) // 2], res[:])
+                    look_up(gathered, t[j], out_l, first, count)
+                    sums = keep.tile([P, count // 2], F32, name="sums%d_%d" % (j, first))
+                    is_last = j == LAST and first + count == EDGES
+                    pair_sum(nc.vector if is_last else nc.gpsimd, sums[:], gathered)
+                    nc.sync.dma_start(out_0[j * P:(j + 1) * P, first // 2:(first + count) // 2], sums[:])
 
-        node_halves([(0, 0), (0, 1), (1, 0)], "first")
+        node_gradients([(0, 0), (0, 1), (1, 0)], "to")
         wi = keep.tile([P, EDGES], F32, name="wi")
         for a in range(2):
-            look_up(half(wi, a), w_row, inn_l, a)
-            gp_pair_sum(sw[:, a * 256:(a + 1) * 256], half(wi, a))
-        node_halves([(1, 1), (2, 0)], "w_row")
+            look_up(half(wi, a), w_row, inn_l, a * HALF)
+            pair_sum(nc.gpsimd, sw[:, a * HALF_NODES:(a + 1) * HALF_NODES], half(wi, a))
+        node_gradients([(1, 1), (2, 0)], "w_row")
         sb = keep.tile([P, EDGES], F32, name="sb")
         for a in range(2):
-            look_up(half(sb, a), sw, dst_l, a)
-            bank = to_columns(half(sb, a), "u%d" % a)
-            for b in range(4):
-                j = 4 * a + b
-                nc.scalar.activation(o1col[:, j:j + 1], bank[:, b, 0:1], ACT.Identity,
-                                     scale=nal_col[:, j:j + 1], bias=w_col[:, j:j + 1])
-        bank = new_bank("u2")
-        nc.tensor.transpose(bank[:, 0, :], o1col[:], ident[:])
-        o1row = keep.tile([8, P], F32, name="o1row")
-        nc.scalar.copy(o1row[:], bank[0:8, 0, :])
-        nc.scalar.dma_start(out_1.rearrange("o (j p) -> (o j) p", p=P), o1row[:])
-        node_halves([(2, 1), (3, 0), (3, 1)], "sw")
+            look_up(half(sb, a), sw, dst_l, a * HALF)
+            sb_bank = turn(half(sb, a), "u%d" % a)
+            for b in range(PER_BANK):
+                k = PER_BANK * a + b
+                nc.scalar.activation(o1_col[:, k:k + 1], sb_bank[:, b, 0:1], ACT.Identity,
+                                     scale=minus_al_col[:, k:k + 1], bias=w_col[:, k:k + 1])
+        o1_bank = new_bank("u2")
+        nc.tensor.transpose(o1_bank[:, 0, :], o1_col[:], ident[:])
+        o1_row = keep.tile([GROUPS, P], F32, name="o1_row")
+        nc.scalar.copy(o1_row[:], o1_bank[0:GROUPS, 0, :])
+        nc.scalar.dma_start(out_1.rearrange("o (k p) -> (o k) p", p=P), o1_row[:])
+        node_gradients([(2, 1), (LAST, 0), (LAST, 1)], "sw")

from contextlib import ExitStack

import concourse.mybir as mybir
from concourse.masks import make_identity

F32 = mybir.dt.float32
BF16 = mybir.dt.bfloat16
U32 = mybir.dt.uint32
U16 = mybir.dt.uint16
U8 = mybir.dt.uint8
E4M3 = mybir.dt.float8_e4m3fn_x4
E5M2 = mybir.dt.float8_e5m2_x4
ACT = mybir.ActivationFunctionType
MULT = mybir.AluOpType.mult
ADD = mybir.AluOpType.add

P = 128
PACK = 4
NODES = 512
EDGES = 1024
HALF = EDGES // 2
HALF_NODES = NODES // 2
BLOCKS = 4
LAST = BLOCKS - 1
GROUPS = EDGES // P
PER_BANK = 4
PER_COLUMN = 16
SPARE = 8
FLOPS = 2 * 512 * 512 * 512


def tile_attend_ggattn_kernel(tc, hT, W, dyT, sc, dstoffs, innoffs, soffs, ooffs, out_0, out_1):
    nc = tc.nc
    with ExitStack() as ctx:
        keep = ctx.enter_context(tc.tile_pool(name="keep", bufs=1))
        psum = ctx.enter_context(tc.psum_pool(name="psum", bufs=1))

        def half(tile, a):
            return tile[:, a * HALF:(a + 1) * HALF]

        def entries(offsets, first, count):
            return offsets[:, first // PER_COLUMN:(first + count) // PER_COLUMN]

        def node_window(name):
            window = keep.tile([P, NODES + SPARE], F32, name=name)
            nc.vector.memset(window[:, NODES:], 0.0)
            return window

        def new_bank(tag):
            return psum.tile([P, PER_BANK, P], F32, name="bank", tag=tag)

        def turn(src, tag):
            bank = new_bank(tag)
            for b in range(PER_BANK):
                nc.tensor.transpose(bank[:, b, :], src[:, b * P:(b + 1) * P], ident[:])
            return bank

        def to_row(row, columns, k0, count, tag):
            bank = new_bank(tag)
            for b in range(count):
                nc.tensor.transpose(bank[:, b, :], columns[:, k0 + b:k0 + b + 1].to_broadcast([P, P]), ident[:])
            nc.scalar.copy(row[:, k0 * P:(k0 + count) * P], bank[:, :count, :].rearrange("p b c -> p (b c)"))

        def pair_sum(engine, dst, gathered):
            engine.tensor_tensor(dst, gathered[:, 0::2], gathered[:, 1::2], ADD)

        def look_up(dst, window, offsets, first, count=HALF):
            nc.vector.tensor_copy(dst, window[:].indirect(entries(offsets, first, count)))

        def look_up_times(dst, window, offsets, first, count, factor):
            nc.vector.tensor_tensor(dst, window[:].indirect(entries(offsets, first, count)), factor, MULT)

        src_l = keep.tile([P, EDGES // PER_COLUMN], U16, name="src_l")
        inn_l = keep.tile([P, EDGES // PER_COLUMN], U16, name="inn_l")
        dst_l = keep.tile([P, EDGES // PER_COLUMN], U16, name="dst_l")
        out_l = keep.tile([P, EDGES // PER_COLUMN], U16, name="out_l")

        o1_col = keep.tile([P, P], F32, name="o1_col")
        filler = (P - GROUPS) // 2
        nc.vector.memset(o1_col[:, GROUPS:GROUPS + filler], 0.0)
        nc.scalar.activation(o1_col[:, GROUPS + filler:], o1_col[:, GROUPS:GROUPS + filler], ACT.Exp)

        e = keep.tile([P, EDGES], F32, name="e")
        nc.vector.memset(e[:], 0.0)
        h = [node_window("h%d" % j) for j in range(BLOCKS)]
        u = [node_window("u%d" % j) for j in range(BLOCKS)]
        den = node_window("den")
        sw = node_window("sw")
        ident = keep.tile([P, P], F32, name="ident")
        make_identity(nc, ident[:])

        sc_row = keep.tile([1, EDGES], F32, name="sc_row", tag="dy_bf", align_bytes=64)
        dy_raw = [keep.tile([P, PACK, HALF_NODES], F32, name="dy_raw%d" % a) for a in range(2)]
        w_raw = [keep.tile([P, PACK, 2 * P], F32, name="w_raw%d" % i) for i in range(2)]
        nc.sync.dma_start(src_l[:], soffs)
        nc.scalar.dma_start(h[0][:, :NODES], hT[0:P, :])
        nc.sync.dma_start(sc_row[:], sc[0:1, :])
        nc.sync.dma_start(h[1][:, :NODES], hT[P:2 * P, :])
        nc.sync.dma_start(inn_l[:], innoffs)
        nc.sync.dma_start(dst_l[:], dstoffs)
        dy_rows = dyT.rearrange("(p r) x -> p r x", r=PACK)
        for a in range(2):
            nc.sync.dma_start(dy_raw[a][:], dy_rows[:, :, a * HALF_NODES:(a + 1) * HALF_NODES])
        nc.sync.dma_start(h[2][:, :NODES], hT[2 * P:3 * P, :])
        w_rows = W.rearrange("(p r) d -> p r d", r=PACK)
        for i in range(2):
            nc.sync.dma_start(w_raw[i][:], w_rows[:, :, i * 2 * P:(i + 1) * 2 * P])
        nc.sync.dma_start(h[LAST][:, :NODES], hT[LAST * P:, :])
        nc.sync.dma_start(out_l[:], ooffs)

        nc.scalar.activation(e[0:1, :], sc_row[:], ACT.Exp)
        e_banks = [turn(half(e, a), ("qa", "qb")[a]) for a in range(2)]
        hs = [keep.tile([P, HALF], F32, name="hs%d" % j) for j in range(LAST)]
        for j in range(2):
            look_up(hs[j][:], h[j], src_l, 0)
        es = keep.tile([P, EDGES], F32, name="es")
        for a in range(2):
            look_up(half(es, a), e, inn_l, a * HALF)
            pair_sum(nc.gpsimd, den[:, a * HALF_NODES:(a + 1) * HALF_NODES], half(es, a))
        look_up(hs[2][:], h[2], src_l, 0)

        al_col = keep.tile([P, GROUPS], F32, name="al_col")
        minus_al_col = keep.tile([P, GROUPS], F32, name="minus_al_col")
        al = keep.tile([P, EDGES], F32, name="al")

        dy_bf = keep.tile([P, NODES, PACK], BF16, name="dy_bf", align_bytes=64)
        for a in range(2):
            nc.scalar.copy(dy_bf[:, a * HALF_NODES:(a + 1) * HALF_NODES, :], dy_raw[a][:].rearrange("p r x -> p x r"))
        dy_q = keep.tile([P, NODES], U32, name="dy_q", align_bytes=64)
        dy_s = keep.tile([P, NODES], U8, name="dy_s", align_bytes=64)
        nc.vector.quantize_mx(out=dy_q[:].bitcast(E5M2), scales=dy_s[:], in_=dy_bf[:].rearrange("p x r -> p (x r)"))

        def products(i):
            w_bf = keep.tile([P, 2 * P, PACK], BF16, name="w_bf%d" % i, align_bytes=64)
            nc.scalar.copy(w_bf[:], w_raw[i][:].rearrange("p r d -> p d r"))
            w_q = keep.tile([P, 2 * P], U32, name="w_q%d" % i, align_bytes=64)
            w_s = keep.tile([P, 2 * P], U8, name="w_s%d" % i, align_bytes=64)
            nc.vector.quantize_mx(out=w_q[:].bitcast(E4M3), scales=w_s[:], in_=w_bf[:].rearrange("p d r -> p (d r)"))
            for b in range(2):
                features = slice(b * P, (b + 1) * P)
                acc = psum.tile([P, NODES], F32, name="acc", tag="u%d" % (2 * i + b))
                nc.tensor.matmul_mx(out=acc[:], lhsT=w_q[:, features].bitcast(E4M3), lhsT_scale=w_s[:, features],
                                    rhs=dy_q[:].bitcast(E5M2), rhs_scale=dy_s[:], start=True, stop=True)
                nc.scalar.copy(u[2 * i + b][:, :NODES], acc[:])

        t = [keep.tile([P, EDGES], F32, name="t%d" % j) for j in range(BLOCKS)]
        q = [keep.tile([P, EDGES], F32, name="q%d" % j) for j in range(BLOCKS)]
        sum_out = keep.tile([P, P], F32, name="sum_out")

        products(0)
        dn = keep.tile([P, EDGES], F32, name="dn", tag="w_bf0", align_bytes=64)
        for a in range(2):
            look_up(half(dn, a), den, dst_l, a * HALF)
        for a in range(2):
            dn_bank = turn(half(dn, a), "xy"[a])
            dn_inverse = keep.tile([P, PER_BANK], F32, name="dn_inverse%d" % a)
            nc.vector.reciprocal(dn_inverse[:], dn_bank[:, :, 0])
            for b in range(PER_BANK):
                k = PER_BANK * a + b
                nc.scalar.activation(al_col[:, k:k + 1], e_banks[a][:, b, 0:1], ACT.Identity,
                                     scale=dn_inverse[:, b:b + 1])
        to_row(al, al_col, PER_BANK, PER_BANK, "u0")
        nc.scalar.mul(minus_al_col[:], al_col[:], -1.0)
        products(1)

        ud = [keep.tile([P, HALF], F32, name="ud%d" % j) for j in range(BLOCKS)]
        for j in range(BLOCKS):
            look_up(ud[j][:], u[j], dst_l, 0)
            if j < LAST:
                nc.gpsimd.tensor_tensor(half(q[j], 0), ud[j][:], hs[j][:], MULT)

        parts = [(0, 4, new_bank("qa"), "u0"), (4, 2, new_bank("qb"), "u2"), (6, 2, new_bank("u1"), "x")]
        w_col = keep.tile([P, GROUPS], F32, name="w_col")
        w_row = keep.tile([P, EDGES], F32, name="w_row")

        def add_up(j, first, count):
            for k0, groups, bank, row_tag in parts:
                if not first <= k0 * P < first + count:
                    continue
                for b in range(groups):
                    c0 = (k0 + b) * P
                    nc.tensor.matmul(bank[:, b, :], q[j][:, c0:c0 + P], ident[:], is_transpose=True,
                                     start=(j == 0 and b == 0), stop=(j == LAST and b == groups - 1))
                if j == LAST:
                    for b in range(groups):
                        k = k0 + b
                        if k0 * P < HALF:
                            nc.scalar.activation(sum_out[:], bank[:, b, :], ACT.Identity, scale=al_col[:, k:k + 1],
                                                 accum_out=w_col[:, k:k + 1])
                        else:
                            nc.scalar.activation(sum_out[:], bank[:, b, :], ACT.Copy, accum_out=w_col[:, k:k + 1])
                    to_row(w_row, w_col, k0, groups, row_tag)

        for j in range(BLOCKS):
            if j == LAST:
                look_up_times(half(q[j], 0), h[j], src_l, 0, HALF, ud[j][:])
            add_up(j, 0, HALF)

        def scale_turned(j, tag):
            bank = turn(ud[j], tag)
            scaled = keep.tile([P, PER_BANK, P], F32, name="scaled%d" % j)
            for b in range(PER_BANK):
                nc.scalar.activation(scaled[:, b, :], bank[:, b, :], ACT.Identity, scale=al_col[:, b:b + 1])
            back = new_bank("u%d" % (2 + j % 2))
            for b in range(PER_BANK):
                nc.tensor.transpose(back[:, b, :], scaled[:, b, :], ident[:])
            nc.scalar.copy(half(t[j], 0), back[:].rearrange("p b c -> p (b c)"))

        for j in range(2):
            scale_turned(j, "xy"[j])

        for pair, count in (((0, 1), HALF), ((2, 3), HALF // 2)):
            for j in pair:
                look_up_times(half(t[j], 1), u[j], dst_l, HALF, HALF, half(al, 1))
            for first in range(HALF, EDGES, count):
                for j in pair:
                    edges = slice(first, first + count)
                    look_up_times(q[j][:, edges], h[j], src_l, first, count, t[j][:, edges])
                    add_up(j, first, count)

        for j in range(2, BLOCKS):
            scale_turned(j, "x")

        def node_gradients(pieces, tag):
            to = keep.tile([P, len(pieces) * HALF], F32, name="to", tag=tag)
            for i, (j, a) in enumerate(pieces):
                count = HALF // 2 if (j, a) == (LAST, 1) else HALF
                for c0 in range(0, HALF, count):
                    gathered = to[:, i * HALF + c0:i * HALF + c0 + count]
                    first = a * HALF + c0
                    look_up(gathered, t[j], out_l, first, count)
                    sums = keep.tile([P, count // 2], F32, name="sums%d_%d" % (j, first))
                    is_last = j == LAST and first + count == EDGES
                    pair_sum(nc.vector if is_last else nc.gpsimd, sums[:], gathered)
                    nc.sync.dma_start(out_0[j * P:(j + 1) * P, first // 2:(first + count) // 2], sums[:])

        node_gradients([(0, 0), (0, 1), (1, 0)], "to")
        wi = keep.tile([P, EDGES], F32, name="wi")
        for a in range(2):
            look_up(half(wi, a), w_row, inn_l, a * HALF)
            pair_sum(nc.gpsimd, sw[:, a * HALF_NODES:(a + 1) * HALF_NODES], half(wi, a))
        node_gradients([(1, 1), (2, 0)], "w_row")
        sb = keep.tile([P, EDGES], F32, name="sb")
        for a in range(2):
            look_up(half(sb, a), sw, dst_l, a * HALF)
            sb_bank = turn(half(sb, a), "u%d" % a)
            for b in range(PER_BANK):
                k = PER_BANK * a + b
                nc.scalar.activation(o1_col[:, k:k + 1], sb_bank[:, b, 0:1], ACT.Identity,
                                     scale=minus_al_col[:, k:k + 1], bias=w_col[:, k:k + 1])
        o1_bank = new_bank("u2")
        nc.tensor.transpose(o1_bank[:, 0, :], o1_col[:], ident[:])
        o1_row = keep.tile([GROUPS, P], F32, name="o1_row")
        nc.scalar.copy(o1_row[:], o1_bank[0:GROUPS, 0, :])
        nc.scalar.dma_start(out_1.rearrange("o (k p) -> (o k) p", p=P), o1_row[:])
        node_gradients([(2, 1), (LAST, 0), (LAST, 1)], "sw")
